import numpy as np
import ml_dtypes


def mxq(x, axis, fmt="e4m3"):
    dtype, down = {"e4m3": (ml_dtypes.float8_e4m3fn, 7), "e5m2": (ml_dtypes.float8_e5m2, 14)}[fmt]
    v = np.moveaxis(np.asarray(x, np.float32).astype(ml_dtypes.bfloat16).astype(np.float64), axis, -1)
    blocks = v.reshape(v.shape[:-1] + (-1, 32))
    amax = np.abs(blocks).max(-1, keepdims=True)
    byte = np.maximum(np.where(amax > 0, np.frexp(amax)[1] - 1 + 127, 0) - down, 1)
    scale = np.exp2(byte - 127.0)
    codes = (blocks / scale).astype(np.float32).astype(dtype).astype(np.float64)
    return np.moveaxis((codes * scale).reshape(v.shape), -1, axis)


WIDE = False


def mx_kscale(k):
    if not WIDE:
        return np.ones(k)
    levels = np.array([10, -10, 5, -5, 0])
    if k % 512:
        return np.exp2(np.random.permutation(np.resize(levels, k // 32))).repeat(32)
    a = np.empty((k // 512, 16))
    for p in range(k // 512):
        a[p, :8] = np.random.permutation(np.resize(levels, 8))
        for g in range(8):
            far = levels[np.abs(levels - a[p, g]) >= 10]
            a[p, g + 8] = far[np.random.randint(len(far))]
    return np.exp2(a.ravel()).repeat(32)


def f64(x):
    return np.asarray(x).astype(np.float64)


def striped(idx):
    return np.tile(idx.reshape(-1, 16).T, (8, 1)).astype(np.uint16)


def unstriped(offs):
    return offs[:16].T.reshape(-1).astype(np.int64)


E2M1 = np.array([0.0, 0.5, 1.0, 1.5, 2.0, 3.0, 4.0, 6.0, -0.0, -0.5, -1.0, -1.5, -2.0, -3.0, -4.0, -6.0])


def pack_weight(w, fmt):
    k, n = w.shape
    w = f64(np.asarray(w, np.float32).astype(ml_dtypes.bfloat16)).reshape(k // 32, 32, n)
    amax = np.abs(w).max(1)
    if fmt == "e4m3":
        byte = np.frexp(amax)[1] - 1 + 127 - 7
    else:
        mant, ex = np.frexp(amax / 6.0)
        byte = np.where(mant > 0.5, ex, ex - 1) + 127
    byte = np.clip(np.where(amax > 0, byte, 1), 1, 254)
    scaled = (w * np.exp2(127.0 - byte)[:, None, :]).reshape(k, n).astype(np.float32)
    by_word = np.ascontiguousarray(scaled.reshape(k // 512, 128, 4, n).transpose(0, 1, 3, 2))
    if fmt == "e4m3":
        words = by_word.astype(ml_dtypes.float8_e4m3fn).view(np.uint8)
    else:
        c = by_word.astype(ml_dtypes.float4_e2m1fn).view(np.uint8) & 0xF
        words = (c[..., 0::2] | (c[..., 1::2] << 4)).reshape(k // 512, 128, 2 * n)
    return np.ascontiguousarray(words), np.ascontiguousarray(byte.astype(np.uint8).reshape(k // 512, 16, n))


def unpack_weight(words, scales, fmt):
    g, _, n = scales.shape
    words = np.ascontiguousarray(words).reshape(g, 128, n, -1)
    if fmt == "e4m3":
        vals = words.view(ml_dtypes.float8_e4m3fn).astype(np.float64)
    else:
        nib = np.empty((g, 128, n, 4), np.uint8)
        nib[..., 0::2] = words & 0xF
        nib[..., 1::2] = words >> 4
        vals = E2M1[nib]
    vals = vals * np.repeat(np.exp2(scales.astype(np.float64) - 127.0), 8, axis=1)[..., None]
    return vals.transpose(0, 1, 3, 2).reshape(g * 512, n)


def d_relu(v):
    return (v > 0).astype(np.float64)


K, T, G, C1, E, C2, H = 512, 1024, 2, 512, 4, 256, 512
N = 1024


def by_expert(wq, xq, E, C):
    return np.concatenate([wq[e].T @ xq[:, e * C:(e + 1) * C] for e in range(E)], axis=1)


def setup_inputs():
    n = np.random.standard_normal
    v = mx_kscale(N)
    u = mx_kscale(H)
    slots1 = np.random.permutation(T)
    slots2 = np.concatenate([q * C1 + np.random.permutation(C1) for q in range(G)])
    dy = pack_weight(n((N, T)) * v[:, None], "e4m3")
    wet = [pack_weight(m, "e2m1") for m in n((E, N, H)) / np.sqrt(N) / v[None, :, None] * u]
    return {
        "dy_words": dy[0],
        "dy_scales": dy[1],
        "wet_words": np.stack([m[0] for m in wet]),
        "wet_scales": np.stack([m[1] for m in wet]),
        "wgt": (n((G, H, K)) / np.sqrt(H) / u[None, :, None]).astype(np.float32),
        "a": (n((H, T))).astype(np.float32),
        "gate": (np.tile(np.random.uniform(0.2, 1.0, T), (128, 1))).astype(np.float32),
        "offs": striped(slots1),
        "offs2": striped(slots2),
        "dst": striped(slots1[slots2]),
    }


def reference(dy_words, dy_scales, wet_words, wet_scales, wgt, a, gate, offs, offs2, dst):
    wet = np.stack([unpack_weight(wet_words[e], wet_scales[e], "e2m1") for e in range(E)])
    wgtq = mxq(f64(wgt), 1, "e4m3")
    gq = unpack_weight(dy_words, dy_scales, "e4m3")[:, unstriped(dst)]
    z = f64(gate[:1]) * by_expert(wet, gq, E, C2)
    da = np.zeros((H, T))
    da[:, unstriped(offs2)] = z
    dx = by_expert(wgtq, mxq(da * d_relu(f64(a)), 0, "e4m3"), G, C1)
    out = np.zeros((K, T))
    out[:, unstriped(offs)] = dx
    return out

@@ -1,0 +1,222 @@
+from contextlib import ExitStack
+
+import concourse.mybir as mybir
+from concourse.masks import make_identity
+
+F32 = mybir.dt.float32
+BF16 = mybir.dt.bfloat16
+I32 = mybir.dt.int32
+U32 = mybir.dt.uint32
+U16 = mybir.dt.uint16
+U8 = mybir.dt.uint8
+FP8X4 = mybir.dt.float8_e4m3fn_x4
+FP4X4 = mybir.dt.float4_e2m1fn_x4
+COPY = mybir.ActivationFunctionType.Copy
+IS_GT = mybir.AluOpType.is_gt
+MULT = mybir.AluOpType.mult
+
+P = 128
+PACK = 4
+K, T, G, C1, E, C2, H, N = 512, 1024, 2, 512, 4, 256, 512, 1024
+PASSES = N // (P * PACK)
+PER_COL = 16
+FLOPS = 2 * N * H * T + 2 * H * K * T
+
+
+def tile_moe_hib_relu_kernel(
+    tc, dy_words, dy_scales, wet_words, wet_scales, wgt, a, gate, offs, offs2, dst, out
+):
+    nc = tc.nc
+    with ExitStack() as ctx:
+        lists = ctx.enter_context(tc.tile_pool(name="lists", bufs=1))
+        keep = ctx.enter_context(tc.tile_pool(name="keep", bufs=1))
+        stage = ctx.enter_context(tc.tile_pool(name="stage", bufs=2))
+        ring = ctx.enter_context(tc.tile_pool(name="ring", bufs=3))
+        psum_z = ctx.enter_context(tc.psum_pool(name="psum_z", bufs=3))
+        psum_t = ctx.enter_context(tc.psum_pool(name="psum_t", bufs=3))
+        psum_x = ctx.enter_context(tc.psum_pool(name="psum_x", bufs=2))
+
+        def entries(offsets, first, last):
+            return offsets[:, first // PER_COL : last // PER_COL]
+
+        dst_sb = lists.tile([P, T // PER_COL], U16, name="dst_sb")
+        offs2_sb = lists.tile([P, T // PER_COL], U16, name="offs2_sb")
+        offs_sb = lists.tile([P, T // PER_COL], U16, name="offs_sb")
+
+        dy_sc = keep.tile([P, T], U8, name="dy_sc", align_bytes=64)
+        slot_sc = keep.tile([P, T], U8, name="slot_sc", align_bytes=64)
+        slot_sc1 = keep.tile([P, T], U8, name="slot_sc1", align_bytes=64)
+        wet_sc = keep.tile([P, E * PASSES, H], U8, name="wet_sc", align_bytes=64)
+        slot_w = keep.tile([P, PASSES, T], U32, name="slot_w", align_bytes=64)
+        gate_rows = keep.tile([P, P], F32, name="gate_rows")
+        gate_col = keep.tile([P, T // P], F32, name="gate_col")
+        ident = keep.tile([P, P], F32, name="ident")
+
+        nc.vector.memset(dy_sc[:].bitcast(I32), 0)
+        nc.vector.memset(wet_sc[:].rearrange("p g h -> p (g h)").bitcast(I32), 0)
+        nc.vector.memset(slot_sc1[:].bitcast(I32), 0)
+        nc.gpsimd.memset(gate_rows[:], 0.0)
+        make_identity(nc, ident[:])
+
+        dy_w = stage.tile([P, PASSES, T], I32, name="dy_w", tag="stage", align_bytes=64)
+        wet_w0 = stage.tile([P, 2 * PASSES, 2 * H], U8, name="wet_w0", tag="stage", align_bytes=64)
+        wet_w1 = keep.tile([P, 2 * PASSES, 2 * H], U8, name="wet_w1", align_bytes=64)
+        wet_w = [wet_w0, wet_w1]
+
+        def load_dy_words(s):
+            nc.sync.dma_start(dy_w[:, s, :], dy_words[s].rearrange("p t d -> p (t d)").bitcast(I32))
+
+        def load_wet_words(f):
+            nc.sync.dma_start(
+                wet_w[f][:].bitcast(I32),
+                wet_words[2 * f : 2 * f + 2].rearrange("e s p c -> p (e s) c").bitcast(I32),
+            )
+
+        nc.sync.dma_start(dst_sb[:], dst)
+        load_dy_words(0)
+        for q in range(4):
+            nc.sync.dma_start(
+                dy_sc[32 * q : 32 * q + 8, :].bitcast(I32),
+                dy_scales[:, 4 * q : 4 * q + 4, :].bitcast(I32),
+            )
+        load_dy_words(1)
+        load_wet_words(0)
+        nc.sync.dma_start(gate_rows[0 : T // P, :], gate[0:1, :].rearrange("o (c p) -> (o c) p", p=P))
+        for q in range(4):
+            nc.sync.dma_start(
+                wet_sc[32 * q : 32 * q + 4, :, :].bitcast(I32),
+                wet_scales[:, :, 4 * q : 4 * q + 4, :].rearrange("e s r h -> r (e s) h").bitcast(I32),
+            )
+        nc.sync.dma_start(offs2_sb[:], offs2)
+        load_wet_words(1)
+
+        gate_ps = psum_t.tile([P, PACK, P], F32, name="gate_ps", tag="turned")
+        nc.tensor.transpose(gate_ps[:, 0, :], gate_rows[:], ident[:])
+        nc.scalar.activation(gate_col[:], gate_ps[:, 0, 0 : T // P], COPY)
+
+        for first, last in ((0, C2), (C2, T)):
+            nc.vector.tensor_copy(slot_sc[:, first:last], dy_sc[:].indirect(entries(dst_sb, first, last)))
+            nc.sync.dma_start(
+                slot_sc1[0:112, first:last].bitcast(I32), slot_sc[4:116, first:last].bitcast(I32)
+            )
+        nc.sync.dma_start(offs_sb[:], offs)
+        pieces = ((0, C2), (C2, C1), (C1, T))
+        for first, last in pieces:
+            for s in range(PASSES):
+                nc.vector.tensor_copy(
+                    slot_w[:, s, first:last],
+                    dy_w[:, s, :].bitcast(U32).indirect(entries(dst_sb, first, last)),
+                )
+
+        z_slots = keep.tile([P, PACK, T], F32, name="z_slots")
+        for st in range(T // P):
+            slots = slice(st * P, (st + 1) * P)
+            e = st * P // C2
+            zt_ps = psum_z.tile([P, H], F32, name="zt_ps")
+            for s in range(PASSES):
+                nc.tensor.matmul_mx(
+                    out=zt_ps[:],
+                    lhsT=slot_w[:, s, slots].bitcast(FP8X4),
+                    lhsT_scale=(slot_sc, slot_sc1)[s][:, slots],
+                    rhs=wet_w[e // 2][:, (e % 2) * PASSES + s, :].bitcast(FP4X4),
+                    rhs_scale=wet_sc[:, e * PASSES + s, :],
+                    start=(s == 0),
+                    stop=(s == PASSES - 1),
+                )
+            zt = ring.tile([P, PACK, P], F32, name="zt")
+            nc.scalar.activation(
+                zt[:], zt_ps[:].rearrange("m (p t) -> m t p", t=PACK), COPY, scale=gate_col[:, st : st + 1]
+            )
+            z_ps = psum_t.tile([P, PACK, P], F32, name="z_ps", tag="turned")
+            for t in range(PACK):
+                nc.tensor.transpose(z_ps[:, t, :], zt[:, t, :], ident[:])
+            nc.scalar.copy(z_slots[:, :, slots], z_ps[:])
+
+        z_back = [[keep.tile([P, T], F32, name="z_back%d%d" % (f, t)) for t in range(PACK)] for f in range(G)]
+        da = keep.tile([P, PACK, T], BF16, name="da")
+        da_words = keep.tile([P, T], U32, name="da_words", align_bytes=64)
+        da_sc = keep.tile([P, T], U8, name="da_sc", align_bytes=64)
+        wgt_words = keep.tile([P, G, K], U32, name="wgt_words", align_bytes=64)
+        wgt_sc = keep.tile([P, G, K], U8, name="wgt_sc", align_bytes=64)
+
+        def interleave(grouped, planes):
+            nc.scalar.copy(
+                grouped.rearrange("p (c i) t -> p c t i", i=4), planes.rearrange("p t (c i) -> p c t i", i=4)
+            )
+
+        def quantize(words, scales, grouped):
+            nc.vector.quantize_mx(
+                out=words.bitcast(FP8X4), scales=scales, in_=grouped[:].rearrange("p c t -> p (c t)")
+            )
+
+        def scatter_z(f, first, last, t):
+            nc.vector.tensor_copy(z_back[f][t][:].indirect(entries(offs2_sb, first, last)), z_slots[:, t, first:last])
+
+        def load_a(f):
+            a_sb = stage.tile([P, PACK, C1], F32, name="a_sb", tag="stage", align_bytes=64)
+            nc.sync.dma_start(a_sb[:], a[:, f * C1 : (f + 1) * C1].rearrange("(p t) j -> p t j", t=PACK))
+            return a_sb
+
+        def prepare_wgt(f):
+            wgt_raw = stage.tile([P, PACK, K], F32, name="wgt_raw", tag="stage", align_bytes=64)
+            nc.sync.dma_start(wgt_raw[:], wgt[f].rearrange("(p t) k -> p t k", t=PACK))
+            wgt_grouped = keep.tile([P, K, PACK], BF16, name="wgt_grouped%d" % f, align_bytes=64)
+            for c in range(0, K, P):
+                interleave(wgt_grouped[:, c : c + P, :], wgt_raw[:, :, c : c + P])
+            return wgt_grouped
+
+        def mask_z(f, a_sb):
+            cols = slice(f * C1, (f + 1) * C1)
+            for t in range(PACK):
+                nc.vector.scalar_tensor_tensor(
+                    da[:, t, cols], a_sb[:, t, :], 0.0, z_back[f][t][:, cols], IS_GT, MULT
+                )
+            da_grouped = keep.tile([P, C1, PACK], BF16, name="da_grouped%d" % f, align_bytes=64)
+            interleave(da_grouped[:], da[:, :, cols])
+            return da_grouped
+
+        dx_back = [keep.tile([P, T], F32, name="dx_back%d" % kt) for kt in range(K // P)]
+        dx = keep.tile([P, G, K // P, C1], F32, name="dx")
+
+        def multiply_wgt(f):
+            cols = slice(f * C1, (f + 1) * C1)
+            for kt in range(K // P):
+                dx_ps = psum_x.tile([P, C1], F32, name="dx_ps")
+                nc.tensor.matmul_mx(
+                    out=dx_ps[:],
+                    lhsT=wgt_words[:, f, kt * P : (kt + 1) * P].bitcast(FP8X4),
+                    lhsT_scale=wgt_sc[:, f, kt * P : (kt + 1) * P],
+                    rhs=da_words[:, cols].bitcast(FP8X4),
+                    rhs_scale=da_sc[:, cols],
+                    start=True,
+                    stop=True,
+                )
+                nc.scalar.copy(dx[:, f, kt, :], dx_ps[:])
+
+        def scatter_dx(f, kt):
+            nc.vector.tensor_copy(
+                dx_back[kt][:].indirect(entries(offs_sb, f * C1, (f + 1) * C1)), dx[:, f, kt, :]
+            )
+
+        a0 = load_a(0)
+        wgt0 = prepare_wgt(0)
+        for first, last in pieces[:2]:
+            for t in range(PACK):
+                scatter_z(0, first, last, t)
+        quantize(wgt_words[:, 0, :], wgt_sc[:, 0, :], wgt0)
+        wgt1 = prepare_wgt(1)
+        da0 = mask_z(0, a0)
+        a1 = load_a(1)
+        quantize(da_words[:, 0:C1], da_sc[:, 0:C1], da0)
+        multiply_wgt(0)
+        for t in range(PACK):
+            scatter_z(1, C1, T, t)
+        quantize(wgt_words[:, 1, :], wgt_sc[:, 1, :], wgt1)
+        da1 = mask_z(1, a1)
+        quantize(da_words[:, C1:T], da_sc[:, C1:T], da1)
+        multiply_wgt(1)
+        for kt in range(K // P):
+            scatter_dx(0, kt)
+        for kt in range(K // P):
+            scatter_dx(1, kt)
+            nc.sync.dma_start(out[kt * P : (kt + 1) * P, :], dx_back[kt][:])

@@ -12,7 +12,8 @@ U8 = mybir.dt.uint8
 FP8X4 = mybir.dt.float8_e4m3fn_x4
 FP4X4 = mybir.dt.float4_e2m1fn_x4
 COPY = mybir.ActivationFunctionType.Copy
-IS_GT = mybir.AluOpType.is_gt
+SIGN = mybir.ActivationFunctionType.Sign
+RELU = mybir.ActivationFunctionType.Relu
 MULT = mybir.AluOpType.mult
 
 P = 128
@@ -43,7 +44,7 @@ def tile_moe_hib_relu_kernel(
         offs2_sb = lists.tile([P, T // PER_COL], U16, name="offs2_sb")
         offs_sb = lists.tile([P, T // PER_COL], U16, name="offs_sb")
 
-        dy_sc = keep.tile([P, T], U8, name="dy_sc", align_bytes=64)
+        dy_sc = keep.tile([P, T], U8, name="dy_sc", tag="early_late", align_bytes=64)
         slot_sc = keep.tile([P, T], U8, name="slot_sc", align_bytes=64)
         slot_sc1 = keep.tile([P, T], U8, name="slot_sc1", align_bytes=64)
         wet_sc = keep.tile([P, E * PASSES, H], U8, name="wet_sc", align_bytes=64)
@@ -52,7 +53,7 @@ def tile_moe_hib_relu_kernel(
         gate_col = keep.tile([P, T // P], F32, name="gate_col")
         ident = keep.tile([P, P], F32, name="ident")
 
-        nc.vector.memset(dy_sc[:].bitcast(I32), 0)
+        nc.gpsimd.memset(dy_sc[:].bitcast(I32), 0)
         nc.vector.memset(wet_sc[:].rearrange("p g h -> p (g h)").bitcast(I32), 0)
         nc.vector.memset(slot_sc1[:].bitcast(I32), 0)
         nc.gpsimd.memset(gate_rows[:], 0.0)
@@ -60,27 +61,27 @@ def tile_moe_hib_relu_kernel(
 
         dy_w = stage.tile([P, PASSES, T], I32, name="dy_w", tag="stage", align_bytes=64)
         wet_w0 = stage.tile([P, 2 * PASSES, 2 * H], U8, name="wet_w0", tag="stage", align_bytes=64)
-        wet_w1 = keep.tile([P, 2 * PASSES, 2 * H], U8, name="wet_w1", align_bytes=64)
-        wet_w = [wet_w0, wet_w1]
+        wet_w = [wet_w0]
 
         def load_dy_words(s):
             nc.sync.dma_start(dy_w[:, s, :], dy_words[s].rearrange("p t d -> p (t d)").bitcast(I32))
 
-        def load_wet_words(f):
+        def load_wet_words(first, last):
             nc.sync.dma_start(
-                wet_w[f][:].bitcast(I32),
-                wet_words[2 * f : 2 * f + 2].rearrange("e s p c -> p (e s) c").bitcast(I32),
+                wet_w[first // 2][:, (first % 2) * PASSES : (first % 2 + last - first) * PASSES, :].bitcast(I32),
+                wet_words[first:last].rearrange("e s p c -> p (e s) c").bitcast(I32),
             )
 
         nc.sync.dma_start(dst_sb[:], dst)
-        load_dy_words(0)
         for q in range(4):
             nc.sync.dma_start(
                 dy_sc[32 * q : 32 * q + 8, :].bitcast(I32),
                 dy_scales[:, 4 * q : 4 * q + 4, :].bitcast(I32),
             )
+        load_dy_words(0)
         load_dy_words(1)
-        load_wet_words(0)
+        load_wet_words(0, 1)
+        load_wet_words(1, 2)
         nc.sync.dma_start(gate_rows[0 : T // P, :], gate[0:1, :].rearrange("o (c p) -> (o c) p", p=P))
         for q in range(4):
             nc.sync.dma_start(
@@ -88,7 +89,6 @@ def tile_moe_hib_relu_kernel(
                 wet_scales[:, :, 4 * q : 4 * q + 4, :].rearrange("e s r h -> r (e s) h").bitcast(I32),
             )
         nc.sync.dma_start(offs2_sb[:], offs2)
-        load_wet_words(1)
 
         gate_ps = psum_t.tile([P, PACK, P], F32, name="gate_ps", tag="turned")
         nc.tensor.transpose(gate_ps[:, 0, :], gate_rows[:], ident[:])
@@ -96,10 +96,12 @@ def tile_moe_hib_relu_kernel(
 
         for first, last in ((0, C2), (C2, T)):
             nc.vector.tensor_copy(slot_sc[:, first:last], dy_sc[:].indirect(entries(dst_sb, first, last)))
-            nc.sync.dma_start(
+            nc.scalar.dma_start(
                 slot_sc1[0:112, first:last].bitcast(I32), slot_sc[4:116, first:last].bitcast(I32)
             )
         nc.sync.dma_start(offs_sb[:], offs)
+        wet_w.append(keep.tile([P, 2 * PASSES, 2 * H], U8, name="wet_w1", tag="early_late", align_bytes=64))
+        load_wet_words(2, 4)
         pieces = ((0, C2), (C2, C1), (C1, T))
         for first, last in pieces:
             for s in range(PASSES):
@@ -155,7 +157,13 @@ def tile_moe_hib_relu_kernel(
         def load_a(f):
             a_sb = stage.tile([P, PACK, C1], F32, name="a_sb", tag="stage", align_bytes=64)
             nc.sync.dma_start(a_sb[:], a[:, f * C1 : (f + 1) * C1].rearrange("(p t) j -> p t j", t=PACK))
-            return a_sb
+            sign = ring.tile([P, PACK, C1], BF16, name="sign", bufs=1)
+            mask = keep.tile([P, PACK, C1], BF16, name="mask%d" % f)
+            for t in range(PACK):
+                nc.scalar.activation(sign[:, t, :], a_sb[:, t, :], SIGN)
+            for t in range(PACK):
+                nc.scalar.activation(mask[:, t, :], sign[:, t, :], RELU)
+            return mask
 
         def prepare_wgt(f):
             wgt_raw = stage.tile([P, PACK, K], F32, name="wgt_raw", tag="stage", align_bytes=64)
@@ -165,12 +173,10 @@ def tile_moe_hib_relu_kernel(
                 interleave(wgt_grouped[:, c : c + P, :], wgt_raw[:, :, c : c + P])
             return wgt_grouped
 
-        def mask_z(f, a_sb):
+        def mask_z(f, mask):
             cols = slice(f * C1, (f + 1) * C1)
             for t in range(PACK):
-                nc.vector.scalar_tensor_tensor(
-                    da[:, t, cols], a_sb[:, t, :], 0.0, z_back[f][t][:, cols], IS_GT, MULT
-                )
+                nc.gpsimd.tensor_tensor(da[:, t, cols], z_back[f][t][:, cols], mask[:, t, :], MULT)
             da_grouped = keep.tile([P, C1, PACK], BF16, name="da_grouped%d" % f, align_bytes=64)
             interleave(da_grouped[:], da[:, :, cols])
             return da_grouped
@@ -198,25 +204,29 @@ def tile_moe_hib_relu_kernel(
                 dx_back[kt][:].indirect(entries(offs_sb, f * C1, (f + 1) * C1)), dx[:, f, kt, :]
             )
 
-        a0 = load_a(0)
+        mask0 = load_a(0)
         wgt0 = prepare_wgt(0)
         for first, last in pieces[:2]:
             for t in range(PACK):
                 scatter_z(0, first, last, t)
-        quantize(wgt_words[:, 0, :], wgt_sc[:, 0, :], wgt0)
+        da0 = mask_z(0, mask0)
+        mask1 = load_a(1)
         wgt1 = prepare_wgt(1)
-        da0 = mask_z(0, a0)
-        a1 = load_a(1)
+        scatter_z(1, C1, T, 0)
+        quantize(wgt_words[:, 0, :], wgt_sc[:, 0, :], wgt0)
+        scatter_z(1, C1, T, 1)
         quantize(da_words[:, 0:C1], da_sc[:, 0:C1], da0)
         multiply_wgt(0)
-        for t in range(PACK):
-            scatter_z(1, C1, T, t)
+        scatter_z(1, C1, T, 2)
         quantize(wgt_words[:, 1, :], wgt_sc[:, 1, :], wgt1)
-        da1 = mask_z(1, a1)
+        scatter_z(1, C1, T, 3)
+        da1 = mask_z(1, mask1)
+        scatter_dx(0, 0)
+        scatter_dx(0, 1)
         quantize(da_words[:, C1:T], da_sc[:, C1:T], da1)
         multiply_wgt(1)
-        for kt in range(K // P):
-            scatter_dx(0, kt)
+        scatter_dx(0, 2)
+        scatter_dx(0, 3)
         for kt in range(K // P):
             scatter_dx(1, kt)
             nc.sync.dma_start(out[kt * P : (kt + 1) * P, :], dx_back[kt][:])

@@ -53,18 +53,17 @@ def tile_moe_hib_relu_kernel(
         gate_col = keep.tile([P, T // P], F32, name="gate_col")
         ident = keep.tile([P, P], F32, name="ident")
 
-        nc.gpsimd.memset(dy_sc[:].bitcast(I32), 0)
         nc.vector.memset(wet_sc[:].rearrange("p g h -> p (g h)").bitcast(I32), 0)
         nc.vector.memset(slot_sc1[:].bitcast(I32), 0)
-        nc.gpsimd.memset(gate_rows[:], 0.0)
+        warm_in = keep.tile([P, 1], F32, name="warm_in")
+        warm_out = keep.tile([P, 1], F32, name="warm_out")
+        nc.gpsimd.memset(warm_in[:], 0.0)
+        nc.scalar.activation(warm_out[:], warm_in[:], COPY)
         make_identity(nc, ident[:])
 
         dy_w = stage.tile([P, PASSES, T], I32, name="dy_w", tag="stage", align_bytes=64)
         wet_w0 = stage.tile([P, 2 * PASSES, 2 * H], U8, name="wet_w0", tag="stage", align_bytes=64)
         wet_w = [wet_w0]
-
-        def load_dy_words(s):
-            nc.sync.dma_start(dy_w[:, s, :], dy_words[s].rearrange("p t d -> p (t d)").bitcast(I32))
 
         def load_wet_words(first, last):
             nc.sync.dma_start(
@@ -72,23 +71,25 @@ def tile_moe_hib_relu_kernel(
                 wet_words[first:last].rearrange("e s p c -> p (e s) c").bitcast(I32),
             )
 
+        dy_rows = dy_scales.rearrange("s b t -> (s b) t").bitcast(I32)
+        nc.sync.dma_start(
+            dy_sc[0:112, :].bitcast(I32), dy_rows[0:28, :].unsqueeze(0).to_broadcast([4, 28, T // 4])
+        )
         nc.sync.dma_start(dst_sb[:], dst)
-        for q in range(4):
-            nc.sync.dma_start(
-                dy_sc[32 * q : 32 * q + 8, :].bitcast(I32),
-                dy_scales[:, 4 * q : 4 * q + 4, :].bitcast(I32),
-            )
-        load_dy_words(0)
-        load_dy_words(1)
+        nc.sync.dma_start(
+            dy_sc[112:128, :].bitcast(I32), dy_rows[28:32, :].unsqueeze(0).to_broadcast([4, 4, T // 4])
+        )
+        nc.sync.dma_start(gate_rows[:], gate[0 : P * P // T, :].rearrange("r (c p) -> (r c) p", p=P))
+        nc.sync.dma_start(offs2_sb[:], offs2)
+        nc.sync.dma_start(offs_sb[:], offs)
+        nc.sync.dma_start(dy_w[:], dy_words.rearrange("s p t d -> p s (t d)").bitcast(I32))
         load_wet_words(0, 1)
         load_wet_words(1, 2)
-        nc.sync.dma_start(gate_rows[0 : T // P, :], gate[0:1, :].rearrange("o (c p) -> (o c) p", p=P))
         for q in range(4):
-            nc.sync.dma_start(
+            nc.scalar.dma_start(
                 wet_sc[32 * q : 32 * q + 4, :, :].bitcast(I32),
                 wet_scales[:, :, 4 * q : 4 * q + 4, :].rearrange("e s r h -> r (e s) h").bitcast(I32),
             )
-        nc.sync.dma_start(offs2_sb[:], offs2)
 
         gate_ps = psum_t.tile([P, PACK, P], F32, name="gate_ps", tag="turned")
         nc.tensor.transpose(gate_ps[:, 0, :], gate_rows[:], ident[:])
@@ -97,13 +98,11 @@ def tile_moe_hib_relu_kernel(
         for first, last in ((0, C2), (C2, T)):
             nc.vector.tensor_copy(slot_sc[:, first:last], dy_sc[:].indirect(entries(dst_sb, first, last)))
             nc.scalar.dma_start(
-                slot_sc1[0:112, first:last].bitcast(I32), slot_sc[4:116, first:last].bitcast(I32)
+                slot_sc1[0:112, first:last].bitcast(I32), slot_sc[16:128, first:last].bitcast(I32)
             )
-        nc.sync.dma_start(offs_sb[:], offs)
         wet_w.append(keep.tile([P, 2 * PASSES, 2 * H], U8, name="wet_w1", tag="early_late", align_bytes=64))
         load_wet_words(2, 4)
-        pieces = ((0, C2), (C2, C1), (C1, T))
-        for first, last in pieces:
+        for first, last in ((0, P), (P, C1), (C1, T)):
             for s in range(PASSES):
                 nc.vector.tensor_copy(
                     slot_w[:, s, first:last],
@@ -206,7 +205,7 @@ def tile_moe_hib_relu_kernel(
 
         mask0 = load_a(0)
         wgt0 = prepare_wgt(0)
-        for first, last in pieces[:2]:
+        for first, last in ((0, P), (P, C2), (C2, C1)):
             for t in range(PACK):
                 scatter_z(0, first, last, t)
         da0 = mask_z(0, mask0)

@@ -48,7 +48,7 @@ def tile_moe_hib_relu_kernel(
         slot_sc = keep.tile([P, T], U8, name="slot_sc", align_bytes=64)
         slot_sc1 = keep.tile([P, T], U8, name="slot_sc1", align_bytes=64)
         wet_sc = keep.tile([P, E * PASSES, H], U8, name="wet_sc", align_bytes=64)
-        slot_w = keep.tile([P, PASSES, T], U32, name="slot_w", align_bytes=64)
+        slot_w = keep.tile([P, PASSES, T], U32, name="slot_w", tag="slot_w", align_bytes=64)
         gate_rows = keep.tile([P, P], F32, name="gate_rows")
         gate_col = keep.tile([P, T // P], F32, name="gate_col")
         ident = keep.tile([P, P], F32, name="ident")
@@ -113,7 +113,7 @@ def tile_moe_hib_relu_kernel(
         for st in range(T // P):
             slots = slice(st * P, (st + 1) * P)
             e = st * P // C2
-            zt_ps = psum_z.tile([P, H], F32, name="zt_ps")
+            zt_ps = psum_z.tile([P, H], F32, name="zt_ps", tag="sums")
             for s in range(PASSES):
                 nc.tensor.matmul_mx(
                     out=zt_ps[:],
@@ -124,21 +124,17 @@ def tile_moe_hib_relu_kernel(
                     start=(s == 0),
                     stop=(s == PASSES - 1),
                 )
-            zt = ring.tile([P, PACK, P], F32, name="zt")
-            nc.scalar.activation(
-                zt[:], zt_ps[:].rearrange("m (p t) -> m t p", t=PACK), COPY, scale=gate_col[:, st : st + 1]
-            )
-            z_ps = psum_t.tile([P, PACK, P], F32, name="z_ps", tag="turned")
-            for t in range(PACK):
-                nc.tensor.transpose(z_ps[:, t, :], zt[:, t, :], ident[:])
-            nc.scalar.copy(z_slots[:, :, slots], z_ps[:])
+            by_plane = zt_ps[:].rearrange("m (p t) -> m t p", t=PACK)
+            for t0, t1 in ((0, 1), (1, PACK)) if st == 0 else ((0, PACK),):
+                zt = ring.tile([P, t1 - t0, P], F32, name="zt")
+                nc.scalar.activation(zt[:], by_plane[:, t0:t1, :], COPY, scale=gate_col[:, st : st + 1])
+                z_ps = psum_t.tile([P, t1 - t0, P], F32, name="z_ps", tag="turned")
+                for t in range(t1 - t0):
+                    nc.tensor.transpose(z_ps[:, t, :], zt[:, t, :], ident[:])
+                nc.scalar.copy(z_slots[:, t0:t1, slots], z_ps[:])
 
-        z_back = [[keep.tile([P, T], F32, name="z_back%d%d" % (f, t)) for t in range(PACK)] for f in range(G)]
-        da = keep.tile([P, PACK, T], BF16, name="da")
-        da_words = keep.tile([P, T], U32, name="da_words", align_bytes=64)
+        z_back, dx_back = {}, {}
         da_sc = keep.tile([P, T], U8, name="da_sc", align_bytes=64)
-        wgt_words = keep.tile([P, G, K], U32, name="wgt_words", align_bytes=64)
-        wgt_sc = keep.tile([P, G, K], U8, name="wgt_sc", align_bytes=64)
 
         def interleave(grouped, planes):
             nc.scalar.copy(
@@ -150,14 +146,17 @@ def tile_moe_hib_relu_kernel(
                 out=words.bitcast(FP8X4), scales=scales, in_=grouped[:].rearrange("p c t -> p (c t)")
             )
 
-        def scatter_z(f, first, last, t):
-            nc.vector.tensor_copy(z_back[f][t][:].indirect(entries(offs2_sb, first, last)), z_slots[:, t, first:last])
+        def scatter_z(f, first, last, t, tag=None):
+            if (f, t) not in z_back:
+                name = "z_back%d%d" % (f, t)
+                z_back[f, t] = keep.tile([P, T], F32, name=name, tag=tag or name, align_bytes=64)
+            nc.vector.tensor_copy(z_back[f, t][:].indirect(entries(offs2_sb, first, last)), z_slots[:, t, first:last])
 
-        def load_a(f):
-            a_sb = stage.tile([P, PACK, C1], F32, name="a_sb", tag="stage", align_bytes=64)
+        def load_a(f, pool, tag):
+            a_sb = pool.tile([P, PACK, C1], F32, name="a_sb", tag=tag, align_bytes=64)
             nc.sync.dma_start(a_sb[:], a[:, f * C1 : (f + 1) * C1].rearrange("(p t) j -> p t j", t=PACK))
             sign = ring.tile([P, PACK, C1], BF16, name="sign", bufs=1)
-            mask = keep.tile([P, PACK, C1], BF16, name="mask%d" % f)
+            mask = keep.tile([P, PACK, C1], BF16, name="mask%d" % f, tag="mask%d" % f, align_bytes=64)
             for t in range(PACK):
                 nc.scalar.activation(sign[:, t, :], a_sb[:, t, :], SIGN)
             for t in range(PACK):
@@ -167,65 +166,76 @@ def tile_moe_hib_relu_kernel(
         def prepare_wgt(f):
             wgt_raw = stage.tile([P, PACK, K], F32, name="wgt_raw", tag="stage", align_bytes=64)
             nc.sync.dma_start(wgt_raw[:], wgt[f].rearrange("(p t) k -> p t k", t=PACK))
-            wgt_grouped = keep.tile([P, K, PACK], BF16, name="wgt_grouped%d" % f, align_bytes=64)
+            wgt_grouped = keep.tile([P, K, PACK], BF16, name="wgt_grouped%d" % f, tag="wgt_grouped%d" % f, align_bytes=64)
             for c in range(0, K, P):
                 interleave(wgt_grouped[:, c : c + P, :], wgt_raw[:, :, c : c + P])
             return wgt_grouped
 
-        def mask_z(f, mask):
+        def mask_z(f, mask, tag):
             cols = slice(f * C1, (f + 1) * C1)
+            da = keep.tile([P, PACK, C1], BF16, name="da%d" % f, tag=tag, align_bytes=64)
             for t in range(PACK):
-                nc.gpsimd.tensor_tensor(da[:, t, cols], z_back[f][t][:, cols], mask[:, t, :], MULT)
-            da_grouped = keep.tile([P, C1, PACK], BF16, name="da_grouped%d" % f, align_bytes=64)
-            interleave(da_grouped[:], da[:, :, cols])
+                nc.gpsimd.tensor_tensor(da[:, t, :], z_back[f, t][:, cols], mask[:, t, :], MULT)
+            da_grouped = keep.tile([P, C1, PACK], BF16, name="da_grouped%d" % f, tag="da_grouped%d" % f, align_bytes=64)
+            interleave(da_grouped[:], da[:])
             return da_grouped
 
-        dx_back = [keep.tile([P, T], F32, name="dx_back%d" % kt) for kt in range(K // P)]
-        dx = keep.tile([P, G, K // P, C1], F32, name="dx")
+        dx = {}
 
-        def multiply_wgt(f):
+        def multiply_wgt(f, wgt_words, wgt_sc, da_words):
             cols = slice(f * C1, (f + 1) * C1)
             for kt in range(K // P):
-                dx_ps = psum_x.tile([P, C1], F32, name="dx_ps")
+                dx_ps = (psum_x, psum_z)[kt // 2].tile([P, C1], F32, name="dx_ps", tag="sums")
                 nc.tensor.matmul_mx(
                     out=dx_ps[:],
-                    lhsT=wgt_words[:, f, kt * P : (kt + 1) * P].bitcast(FP8X4),
-                    lhsT_scale=wgt_sc[:, f, kt * P : (kt + 1) * P],
-                    rhs=da_words[:, cols].bitcast(FP8X4),
+                    lhsT=wgt_words[:, kt * P : (kt + 1) * P].bitcast(FP8X4),
+                    lhsT_scale=wgt_sc[:, kt * P : (kt + 1) * P],
+                    rhs=da_words[:].bitcast(FP8X4),
                     rhs_scale=da_sc[:, cols],
                     start=True,
                     stop=True,
                 )
-                nc.scalar.copy(dx[:, f, kt, :], dx_ps[:])
+                name = "dx%d%d" % (f, kt)
+                dx[f, kt] = keep.tile([P, C1], F32, name=name, tag=name, align_bytes=64)
+                nc.scalar.copy(dx[f, kt][:], dx_ps[:])
 
-        def scatter_dx(f, kt):
+        def scatter_dx(f, kt, tag=None):
+            if kt not in dx_back:
+                name = "dx_back%d" % kt
+                dx_back[kt] = keep.tile([P, T], F32, name=name, tag=tag or name, align_bytes=64)
             nc.vector.tensor_copy(
-                dx_back[kt][:].indirect(entries(offs_sb, f * C1, (f + 1) * C1)), dx[:, f, kt, :]
+                dx_back[kt][:].indirect(entries(offs_sb, f * C1, (f + 1) * C1)), dx[f, kt][:]
             )
 
-        mask0 = load_a(0)
+        mask0 = load_a(0, stage, "stage")
         wgt0 = prepare_wgt(0)
         for first, last in ((0, P), (P, C2), (C2, C1)):
             for t in range(PACK):
                 scatter_z(0, first, last, t)
-        da0 = mask_z(0, mask0)
-        mask1 = load_a(1)
-        wgt1 = prepare_wgt(1)
+        da0 = mask_z(0, mask0, "da0")
+        mask1 = load_a(1, keep, "slot_w")
         scatter_z(1, C1, T, 0)
-        quantize(wgt_words[:, 0, :], wgt_sc[:, 0, :], wgt0)
         scatter_z(1, C1, T, 1)
-        quantize(da_words[:, 0:C1], da_sc[:, 0:C1], da0)
-        multiply_wgt(0)
         scatter_z(1, C1, T, 2)
-        quantize(wgt_words[:, 1, :], wgt_sc[:, 1, :], wgt1)
-        scatter_z(1, C1, T, 3)
-        da1 = mask_z(1, mask1)
+        wgt_words0 = keep.tile([P, K], U32, name="wgt_words0", align_bytes=64)
+        wgt_sc0 = keep.tile([P, K], U8, name="wgt_sc0", tag="mask0", align_bytes=64)
+        quantize(wgt_words0[:], wgt_sc0[:], wgt0)
+        da_words0 = keep.tile([P, C1], U32, name="da_words0", tag="da_words0", align_bytes=64)
+        quantize(da_words0[:], da_sc[:, 0:C1], da0)
+        multiply_wgt(0, wgt_words0, wgt_sc0, da_words0)
+        scatter_z(1, C1, T, 3, "da_grouped0")
+        wgt1 = prepare_wgt(1)
+        da1 = mask_z(1, mask1, "da_words0")
         scatter_dx(0, 0)
         scatter_dx(0, 1)
-        quantize(da_words[:, C1:T], da_sc[:, C1:T], da1)
-        multiply_wgt(1)
         scatter_dx(0, 2)
-        scatter_dx(0, 3)
+        wgt_words1 = keep.tile([P, K], U32, name="wgt_words1", align_bytes=64)
+        wgt_sc1 = keep.tile([P, K], U8, name="wgt_sc1", tag="mask1", align_bytes=64)
+        quantize(wgt_words1[:], wgt_sc1[:], wgt1)
+        da_words1 = keep.tile([P, C1], U32, name="da_words1", align_bytes=64)
+        quantize(da_words1[:], da_sc[:, C1:T], da1)
+        multiply_wgt(1, wgt_words1, wgt_sc1, da_words1)
+        scatter_dx(0, 3, "da_grouped1")
         for kt in range(K // P):
             scatter_dx(1, kt)
             nc.sync.dma_start(out[kt * P : (kt + 1) * P, :], dx_back[kt][:])

from contextlib import ExitStack

import concourse.mybir as mybir
from concourse.masks import make_identity

F32 = mybir.dt.float32
BF16 = mybir.dt.bfloat16
I32 = mybir.dt.int32
U32 = mybir.dt.uint32
U16 = mybir.dt.uint16
U8 = mybir.dt.uint8
FP8X4 = mybir.dt.float8_e4m3fn_x4
FP4X4 = mybir.dt.float4_e2m1fn_x4
COPY = mybir.ActivationFunctionType.Copy
SIGN = mybir.ActivationFunctionType.Sign
RELU = mybir.ActivationFunctionType.Relu
MULT = mybir.AluOpType.mult

P = 128
PACK = 4
K, T, G, C1, E, C2, H, N = 512, 1024, 2, 512, 4, 256, 512, 1024
PASSES = N // (P * PACK)
PER_COL = 16
FLOPS = 2 * N * H * T + 2 * H * K * T


def tile_moe_hib_relu_kernel(
    tc, dy_words, dy_scales, wet_words, wet_scales, wgt, a, gate, offs, offs2, dst, out
):
    nc = tc.nc
    with ExitStack() as ctx:
        lists = ctx.enter_context(tc.tile_pool(name="lists", bufs=1))
        keep = ctx.enter_context(tc.tile_pool(name="keep", bufs=1))
        stage = ctx.enter_context(tc.tile_pool(name="stage", bufs=2))
        ring = ctx.enter_context(tc.tile_pool(name="ring", bufs=3))
        psum_z = ctx.enter_context(tc.psum_pool(name="psum_z", bufs=3))
        psum_t = ctx.enter_context(tc.psum_pool(name="psum_t", bufs=3))
        psum_x = ctx.enter_context(tc.psum_pool(name="psum_x", bufs=2))

        def entries(offsets, first, last):
            return offsets[:, first // PER_COL : last // PER_COL]

        dst_sb = lists.tile([P, T // PER_COL], U16, name="dst_sb")
        offs2_sb = lists.tile([P, T // PER_COL], U16, name="offs2_sb")
        offs_sb = lists.tile([P, T // PER_COL], U16, name="offs_sb")

        dy_sc = keep.tile([P, T], U8, name="dy_sc", tag="early_late", align_bytes=64)
        slot_sc = keep.tile([P, T], U8, name="slot_sc", align_bytes=64)
        slot_sc1 = keep.tile([P, T], U8, name="slot_sc1", align_bytes=64)
        wet_sc = keep.tile([P, E * PASSES, H], U8, name="wet_sc", align_bytes=64)
        slot_w = keep.tile([P, PASSES, T], U32, name="slot_w", tag="slot_w", align_bytes=64)
        gate_rows = keep.tile([P, P], F32, name="gate_rows")
        gate_col = keep.tile([P, T // P], F32, name="gate_col")
        ident = keep.tile([P, P], F32, name="ident")

        nc.vector.memset(wet_sc[:].rearrange("p g h -> p (g h)").bitcast(I32), 0)
        nc.vector.memset(slot_sc1[:].bitcast(I32), 0)
        warm_in = keep.tile([P, 1], F32, name="warm_in")
        warm_out = keep.tile([P, 1], F32, name="warm_out")
        nc.gpsimd.memset(warm_in[:], 0.0)
        nc.scalar.activation(warm_out[:], warm_in[:], COPY)
        make_identity(nc, ident[:])

        dy_w = stage.tile([P, PASSES, T], I32, name="dy_w", tag="stage", align_bytes=64)
        wet_w0 = stage.tile([P, 2 * PASSES, 2 * H], U8, name="wet_w0", tag="stage", align_bytes=64)
        wet_w = [wet_w0]

        def load_wet_words(first, last):
            nc.sync.dma_start(
                wet_w[first // 2][:, (first % 2) * PASSES : (first % 2 + last - first) * PASSES, :].bitcast(I32),
                wet_words[first:last].rearrange("e s p c -> p (e s) c").bitcast(I32),
            )

        dy_rows = dy_scales.rearrange("s b t -> (s b) t").bitcast(I32)
        nc.sync.dma_start(
            dy_sc[0:112, :].bitcast(I32), dy_rows[0:28, :].unsqueeze(0).to_broadcast([4, 28, T // 4])
        )
        nc.sync.dma_start(dst_sb[:], dst)
        nc.sync.dma_start(
            dy_sc[112:128, :].bitcast(I32), dy_rows[28:32, :].unsqueeze(0).to_broadcast([4, 4, T // 4])
        )
        nc.sync.dma_start(gate_rows[:], gate[0 : P * P // T, :].rearrange("r (c p) -> (r c) p", p=P))
        nc.sync.dma_start(offs2_sb[:], offs2)
        nc.sync.dma_start(offs_sb[:], offs)
        nc.sync.dma_start(dy_w[:], dy_words.rearrange("s p t d -> p s (t d)").bitcast(I32))
        load_wet_words(0, 1)
        load_wet_words(1, 2)
        for q in range(4):
            nc.scalar.dma_start(
                wet_sc[32 * q : 32 * q + 4, :, :].bitcast(I32),
                wet_scales[:, :, 4 * q : 4 * q + 4, :].rearrange("e s r h -> r (e s) h").bitcast(I32),
            )

        gate_ps = psum_t.tile([P, PACK, P], F32, name="gate_ps", tag="turned")
        nc.tensor.transpose(gate_ps[:, 0, :], gate_rows[:], ident[:])
        nc.scalar.activation(gate_col[:], gate_ps[:, 0, 0 : T // P], COPY)

        for first, last in ((0, C2), (C2, T)):
            nc.vector.tensor_copy(slot_sc[:, first:last], dy_sc[:].indirect(entries(dst_sb, first, last)))
            nc.scalar.dma_start(
                slot_sc1[0:112, first:last].bitcast(I32), slot_sc[16:128, first:last].bitcast(I32)
            )
        wet_w.append(keep.tile([P, 2 * PASSES, 2 * H], U8, name="wet_w1", tag="early_late", align_bytes=64))
        load_wet_words(2, 4)
        for first, last in ((0, P), (P, C1), (C1, T)):
            for s in range(PASSES):
                nc.vector.tensor_copy(
                    slot_w[:, s, first:last],
                    dy_w[:, s, :].bitcast(U32).indirect(entries(dst_sb, first, last)),
                )

        z_slots = keep.tile([P, PACK, T], F32, name="z_slots")
        for st in range(T // P):
            slots = slice(st * P, (st + 1) * P)
            e = st * P // C2
            zt_ps = psum_z.tile([P, H], F32, name="zt_ps", tag="sums")
            for s in range(PASSES):
                nc.tensor.matmul_mx(
                    out=zt_ps[:],
                    lhsT=slot_w[:, s, slots].bitcast(FP8X4),
                    lhsT_scale=(slot_sc, slot_sc1)[s][:, slots],
                    rhs=wet_w[e // 2][:, (e % 2) * PASSES + s, :].bitcast(FP4X4),
                    rhs_scale=wet_sc[:, e * PASSES + s, :],
                    start=(s == 0),
                    stop=(s == PASSES - 1),
                )
            by_plane = zt_ps[:].rearrange("m (p t) -> m t p", t=PACK)
            for t0, t1 in ((0, 1), (1, PACK)) if st == 0 else ((0, PACK),):
                zt = ring.tile([P, t1 - t0, P], F32, name="zt")
                nc.scalar.activation(zt[:], by_plane[:, t0:t1, :], COPY, scale=gate_col[:, st : st + 1])
                z_ps = psum_t.tile([P, t1 - t0, P], F32, name="z_ps", tag="turned")
                for t in range(t1 - t0):
                    nc.tensor.transpose(z_ps[:, t, :], zt[:, t, :], ident[:])
                nc.scalar.copy(z_slots[:, t0:t1, slots], z_ps[:])

        z_back, dx_back = {}, {}
        da_sc = keep.tile([P, T], U8, name="da_sc", align_bytes=64)

        def interleave(grouped, planes):
            nc.scalar.copy(
                grouped.rearrange("p (c i) t -> p c t i", i=4), planes.rearrange("p t (c i) -> p c t i", i=4)
            )

        def quantize(words, scales, grouped):
            nc.vector.quantize_mx(
                out=words.bitcast(FP8X4), scales=scales, in_=grouped[:].rearrange("p c t -> p (c t)")
            )

        def scatter_z(f, first, last, t, tag=None):
            if (f, t) not in z_back:
                name = "z_back%d%d" % (f, t)
                z_back[f, t] = keep.tile([P, T], F32, name=name, tag=tag or name, align_bytes=64)
            nc.vector.tensor_copy(z_back[f, t][:].indirect(entries(offs2_sb, first, last)), z_slots[:, t, first:last])

        def load_a(f, pool, tag):
            a_sb = pool.tile([P, PACK, C1], F32, name="a_sb", tag=tag, align_bytes=64)
            nc.sync.dma_start(a_sb[:], a[:, f * C1 : (f + 1) * C1].rearrange("(p t) j -> p t j", t=PACK))
            sign = ring.tile([P, PACK, C1], BF16, name="sign", bufs=1)
            mask = keep.tile([P, PACK, C1], BF16, name="mask%d" % f, tag="mask%d" % f, align_bytes=64)
            for t in range(PACK):
                nc.scalar.activation(sign[:, t, :], a_sb[:, t, :], SIGN)
            for t in range(PACK):
                nc.scalar.activation(mask[:, t, :], sign[:, t, :], RELU)
            return mask

        def prepare_wgt(f):
            wgt_raw = stage.tile([P, PACK, K], F32, name="wgt_raw", tag="stage", align_bytes=64)
            nc.sync.dma_start(wgt_raw[:], wgt[f].rearrange("(p t) k -> p t k", t=PACK))
            wgt_grouped = keep.tile([P, K, PACK], BF16, name="wgt_grouped%d" % f, tag="wgt_grouped%d" % f, align_bytes=64)
            for c in range(0, K, P):
                interleave(wgt_grouped[:, c : c + P, :], wgt_raw[:, :, c : c + P])
            return wgt_grouped

        def mask_z(f, mask, tag):
            cols = slice(f * C1, (f + 1) * C1)
            da = keep.tile([P, PACK, C1], BF16, name="da%d" % f, tag=tag, align_bytes=64)
            for t in range(PACK):
                nc.gpsimd.tensor_tensor(da[:, t, :], z_back[f, t][:, cols], mask[:, t, :], MULT)
            da_grouped = keep.tile([P, C1, PACK], BF16, name="da_grouped%d" % f, tag="da_grouped%d" % f, align_bytes=64)
            interleave(da_grouped[:], da[:])
            return da_grouped

        dx = {}

        def multiply_wgt(f, wgt_words, wgt_sc, da_words):
            cols = slice(f * C1, (f + 1) * C1)
            for kt in range(K // P):
                dx_ps = (psum_x, psum_z)[kt // 2].tile([P, C1], F32, name="dx_ps", tag="sums")
                nc.tensor.matmul_mx(
                    out=dx_ps[:],
                    lhsT=wgt_words[:, kt * P : (kt + 1) * P].bitcast(FP8X4),
                    lhsT_scale=wgt_sc[:, kt * P : (kt + 1) * P],
                    rhs=da_words[:].bitcast(FP8X4),
                    rhs_scale=da_sc[:, cols],
                    start=True,
                    stop=True,
                )
                name = "dx%d%d" % (f, kt)
                dx[f, kt] = keep.tile([P, C1], F32, name=name, tag=name, align_bytes=64)
                nc.scalar.copy(dx[f, kt][:], dx_ps[:])

        def scatter_dx(f, kt, tag=None):
            if kt not in dx_back:
                name = "dx_back%d" % kt
                dx_back[kt] = keep.tile([P, T], F32, name=name, tag=tag or name, align_bytes=64)
            nc.vector.tensor_copy(
                dx_back[kt][:].indirect(entries(offs_sb, f * C1, (f + 1) * C1)), dx[f, kt][:]
            )

        mask0 = load_a(0, stage, "stage")
        wgt0 = prepare_wgt(0)
        for first, last in ((0, P), (P, C2), (C2, C1)):
            for t in range(PACK):
                scatter_z(0, first, last, t)
        da0 = mask_z(0, mask0, "da0")
        mask1 = load_a(1, keep, "slot_w")
        scatter_z(1, C1, T, 0)
        scatter_z(1, C1, T, 1)
        scatter_z(1, C1, T, 2)
        wgt_words0 = keep.tile([P, K], U32, name="wgt_words0", align_bytes=64)
        wgt_sc0 = keep.tile([P, K], U8, name="wgt_sc0", tag="mask0", align_bytes=64)
        quantize(wgt_words0[:], wgt_sc0[:], wgt0)
        da_words0 = keep.tile([P, C1], U32, name="da_words0", tag="da_words0", align_bytes=64)
        quantize(da_words0[:], da_sc[:, 0:C1], da0)
        multiply_wgt(0, wgt_words0, wgt_sc0, da_words0)
        scatter_z(1, C1, T, 3, "da_grouped0")
        wgt1 = prepare_wgt(1)
        da1 = mask_z(1, mask1, "da_words0")
        scatter_dx(0, 0)
        scatter_dx(0, 1)
        scatter_dx(0, 2)
        wgt_words1 = keep.tile([P, K], U32, name="wgt_words1", align_bytes=64)
        wgt_sc1 = keep.tile([P, K], U8, name="wgt_sc1", tag="mask1", align_bytes=64)
        quantize(wgt_words1[:], wgt_sc1[:], wgt1)
        da_words1 = keep.tile([P, C1], U32, name="da_words1", align_bytes=64)
        quantize(da_words1[:], da_sc[:, C1:T], da1)
        multiply_wgt(1, wgt_words1, wgt_sc1, da_words1)
        scatter_dx(0, 3, "da_grouped1")
        for kt in range(K // P):
            scatter_dx(1, kt)
            nc.sync.dma_start(out[kt * P : (kt + 1) * P, :], dx_back[kt][:])
